import numpy as np
import ml_dtypes


def mxq(x, axis, fmt="e4m3"):
    dtype, down = {"e4m3": (ml_dtypes.float8_e4m3fn, 7), "e5m2": (ml_dtypes.float8_e5m2, 14)}[fmt]
    v = np.moveaxis(np.asarray(x, np.float32).astype(ml_dtypes.bfloat16).astype(np.float64), axis, -1)
    blocks = v.reshape(v.shape[:-1] + (-1, 32))
    amax = np.abs(blocks).max(-1, keepdims=True)
    byte = np.maximum(np.where(amax > 0, np.frexp(amax)[1] - 1 + 127, 0) - down, 1)
    scale = np.exp2(byte - 127.0)
    codes = (blocks / scale).astype(np.float32).astype(dtype).astype(np.float64)
    return np.moveaxis((codes * scale).reshape(v.shape), -1, axis)


WIDE = False


def mx_kscale(k):
    if not WIDE:
        return np.ones(k)
    levels = np.array([10, -10, 5, -5, 0])
    if k % 512:
        return np.exp2(np.random.permutation(np.resize(levels, k // 32))).repeat(32)
    a = np.empty((k // 512, 16))
    for p in range(k // 512):
        a[p, :8] = np.random.permutation(np.resize(levels, 8))
        for g in range(8):
            far = levels[np.abs(levels - a[p, g]) >= 10]
            a[p, g + 8] = far[np.random.randint(len(far))]
    return np.exp2(a.ravel()).repeat(32)


def f64(x):
    return np.asarray(x).astype(np.float64)


def striped(idx):
    return np.tile(idx.reshape(-1, 16).T, (8, 1)).astype(np.uint16)


def unstriped(offs):
    return offs[:16].T.reshape(-1).astype(np.int64)


def striped8(idx):
    return np.concatenate([x.reshape(-1, 16).T for x in idx]).astype(np.uint16)


def runs(offs, k):
    lists = np.stack([offs[16 * r : 16 * r + 16].T.reshape(-1) for r in range(8)]).astype(np.int64)
    return lists[np.arange(k) % 512 // 64]


def pack_weight(w):
    k, n = w.shape
    w = f64(np.asarray(w, np.float32).astype(ml_dtypes.bfloat16)).reshape(k // 32, 32, n)
    amax = np.abs(w).max(1)
    byte = np.clip(np.where(amax > 0, np.frexp(amax)[1] - 1 + 127 - 7, 1), 1, 254)
    scaled = (w * np.exp2(127.0 - byte)[:, None, :]).reshape(k, n).astype(np.float32)
    words = np.ascontiguousarray(scaled.reshape(k // 512, 128, 4, n).transpose(0, 1, 3, 2)).astype(ml_dtypes.float8_e4m3fn).view(np.uint8)
    return words, np.ascontiguousarray(byte.astype(np.uint8).reshape(k // 512, 16, n))


def unpack_weight(words, scales):
    g, p, n, _ = words.shape
    vals = np.ascontiguousarray(words).view(ml_dtypes.float8_e4m3fn).astype(np.float64) * np.repeat(np.exp2(scales.astype(np.float64) - 127.0), 8, axis=1)[..., None]
    return vals.transpose(0, 1, 3, 2).reshape(g * 512, n)


def sigmoid(v):
    return 1.0 / (1.0 + np.exp(-np.maximum(v, -700.0)))


K, T, S, N, H, G = 512, 1024, 512, 512, 512, 2048


def setup_inputs():
    n = np.random.standard_normal
    s = mx_kscale(K)[:, None]
    u = mx_kscale(S)
    packed_xT = pack_weight(n((K, T)) * s)
    packed_dT = pack_weight(n((K, G)) / s)
    return {
        "x_words": packed_xT[0],
        "x_scales": packed_xT[1],
        "w1": (n((K, H)) / np.sqrt(K) / s).astype(np.float32),
        "d_words": packed_dT[0],
        "d_scales": packed_dT[1],
        "gn": (np.random.uniform(0.5, 1.5, (H, 1)) * u[:, None]).astype(np.float32),
        "gk": (np.random.uniform(0.5, 1.5, (H, 1)) * u[:, None]).astype(np.float32),
        "w2": (n((H, N)) / np.sqrt(2 * H) / u[:, None]).astype(np.float32),
        "w3": (n((H, N)) / np.sqrt(2 * H) / u[:, None]).astype(np.float32),
        "offs": striped(np.random.permutation(T)[:S]),
        "kidx": striped8(np.random.randint(0, G, (8, H))),
        "two": striped(np.random.permutation(T)[:S]),
        "n1": striped8(np.stack([np.random.permutation(S) for _ in range(8)])),
        "n2": striped8(np.stack([np.random.permutation(S) for _ in range(8)])),
        "n3": striped(np.random.permutation(S)),
        "n4": striped(np.random.permutation(S)),
        "n5": striped(np.random.permutation(S)),
        "n6": striped(np.random.permutation(S)),
        "n7": striped(np.random.permutation(S)),
    }


def reference(x_words, x_scales, w1, d_words, d_scales, gn, gk, w2, w3, offs, kidx, two, n1, n2, n3, n4, n5, n6, n7):
    xq = unpack_weight(x_words, x_scales)[:, unstriped(offs)]
    y = mxq(f64(w1), 0, "e4m3").T @ xq
    z = f64(gn) * (y + (sigmoid(y[np.arange(H)[:, None], runs(n1, H)])) * (y[np.arange(H)[:, None], runs(n2, H)] - y))
    d_kidx = unpack_weight(d_words, d_scales)[np.arange(K)[:, None], runs(kidx, K)]
    x_two = unpack_weight(x_words, x_scales)[:, unstriped(two)]
    s = 0.0625 * (d_kidx.T @ x_two)
    st = s + 0.5 * s[:, unstriped(n3)]
    z2 = f64(gk) * (st - st[:, unstriped(n4)])
    h = mxq(f64(w2), 0, "e4m3").T @ mxq(z, 0, "e4m3") + mxq(f64(w3), 0, "e4m3").T @ mxq(z2, 0, "e4m3")
    return h[:, unstriped(n5)] * sigmoid(h) + h[:, unstriped(n6)] * (sigmoid(h[:, unstriped(n7)]))

@@ -1,0 +1,281 @@
+from contextlib import ExitStack
+
+import concourse.mybir as mybir
+
+F32 = mybir.dt.float32
+BF16 = mybir.dt.bfloat16
+I32 = mybir.dt.int32
+U32 = mybir.dt.uint32
+U16 = mybir.dt.uint16
+U8 = mybir.dt.uint8
+FP8X4 = mybir.dt.float8_e4m3fn_x4
+ACT = mybir.ActivationFunctionType
+ALU = mybir.AluOpType
+
+P = 128
+PACK = 4
+K = 512
+T = 1024
+G = 2048
+S = 512
+HALF = S // 2
+WIN = 2 * S
+LIST_COLS = S // 16
+
+FLOPS = 4 * 2 * 512 * 512 * 512
+
+
+def tile_picked_jkeytrackhopwsum_none_p_kernel(
+    tc, x_words, x_scales, w1, d_words, d_scales, gn, gk, w2, w3, offs, kidx, two, n1, n2, n3, n4, n5, n6, n7, out
+):
+    nc = tc.nc
+    with ExitStack() as ctx:
+        lists = ctx.enter_context(tc.tile_pool(name="lists", bufs=1))
+        keep = ctx.enter_context(tc.tile_pool(name="keep", bufs=1))
+        ring = ctx.enter_context(tc.tile_pool(name="ring", bufs=2))
+        psum = ctx.enter_context(tc.psum_pool(name="psum", bufs=1))
+
+        def sb(name, shape, dtype):
+            return keep.tile(shape, dtype, name=name, align_bytes=64)
+
+        def load_list(name, src):
+            t = lists.tile([P, LIST_COLS], U16, name=name)
+            nc.sync.dma_start(t[:], src)
+            return t
+
+        def cols(c):
+            return slice(c * HALF, (c + 1) * HALF)
+
+        def half_list(lst, c):
+            return lst[:, c * (LIST_COLS // 2) : (c + 1) * (LIST_COLS // 2)]
+
+        def load_weight(name, w, c0, c1):
+            raw = sb(name, [P, PACK, c1 - c0], F32)
+            nc.sync.dma_start(raw[:], w.rearrange("(p j) n -> p j n", j=PACK)[:, :, c0:c1])
+            return raw
+
+        def quantize(codes, scales, grouped, c0, c1):
+            nc.vector.quantize_mx(
+                out=codes[:, c0:c1].bitcast(FP8X4),
+                scales=scales[:, c0:c1],
+                in_=grouped[:, c0:c1, :].rearrange("p n j -> p (n j)"),
+            )
+
+        def weave(grouped):
+            return grouped.rearrange("p (c i) t -> p c t i", i=4)
+
+        def planes(four):
+            return four.rearrange("p t (c i) -> p c t i", i=4)
+
+        ds_tab = sb("ds_tab", [P, G], U8)
+        xs_tab = sb("xs_tab", [P, T], U8)
+        key_scales = sb("key_scales", [P, S], U8)
+        nc.gpsimd.memset(ds_tab[:].bitcast(I32), 0)
+        nc.gpsimd.memset(key_scales[:].bitcast(I32), 0)
+
+        l_offs = load_list("l_offs", offs)
+        for q in range(4):
+            rows = x_scales[0, 4 * q : 4 * q + 4, :].bitcast(I32)
+            nc.sync.dma_start(xs_tab[32 * q : 32 * q + 32, :].bitcast(I32), rows.partition_broadcast(8))
+        l_two = load_list("l_two", two)
+        w1_raw = [load_weight("w1_raw0", w1, 0, HALF)]
+        xw_tab = sb("xw_tab", [P, T], U32)
+        nc.sync.dma_start(xw_tab[:].bitcast(I32), x_words[0].rearrange("p n t -> p (n t)").bitcast(I32))
+        w1_raw.append(load_weight("w1_raw1", w1, HALF, S))
+        l_kidx = load_list("l_kidx", kidx)
+        nc.sync.dma_start(ds_tab[0:P:8, :].bitcast(I32), d_scales[0].bitcast(I32))
+        gn_sb = sb("gn_sb", [P, PACK], F32)
+        nc.sync.dma_start(gn_sb[:], gn.rearrange("(p t) o -> p (t o)", t=PACK))
+        l_n1 = load_list("l_n1", n1)
+        w3_raw = [load_weight("w3_raw%d" % c, w3, c * HALF, (c + 1) * HALF) for c in range(2)]
+        dw_tab = sb("dw_tab", [P, G], U32)
+        nc.sync.dma_start(dw_tab[:].bitcast(I32), d_words[0].rearrange("p n t -> p (n t)").bitcast(I32))
+
+        w1_bf = keep.tile([P, S, PACK], BF16, name="w1_bf", tag="w1_bf", align_bytes=64)
+        w1_view = w1_bf[:].rearrange("p (t m) j -> p m j t", t=PACK)
+        for c in range(2):
+            nc.scalar.copy(w1_view[:, c * 64 : (c + 1) * 64], w1_raw[c][:].rearrange("p j (m t) -> p m j t", t=PACK))
+        x1_scales = sb("x1_scales", [P, S], U8)
+        nc.vector.tensor_copy(x1_scales[:], xs_tab[:].indirect(l_offs[:]))
+        x2_scales = sb("x2_scales", [P, S], U8)
+        nc.vector.tensor_copy(x2_scales[:], xs_tab[:].indirect(l_two[:]))
+        x1_words = sb("x1_words", [P, S], U32)
+        nc.vector.tensor_copy(x1_words[:], xw_tab[:].indirect(l_offs[:]))
+        ds_got = sb("ds_got", [P, S], U8)
+        nc.vector.tensor_copy(ds_got[:], ds_tab[:].indirect(l_kidx[:]))
+        w1_codes = sb("w1_codes", [P, S], U32)
+        w1_scales = sb("w1_scales", [P, S], U8)
+        quantize(w1_codes, w1_scales, w1_bf, 0, S)
+
+        def product(acc, lhs_codes, lhs_scales, t, rhs_codes, rhs_scales, start, stop):
+            m = slice(t * P, (t + 1) * P)
+            nc.tensor.matmul_mx(
+                out=acc,
+                lhsT=lhs_codes[:, m].bitcast(FP8X4),
+                lhsT_scale=lhs_scales[:, m],
+                rhs=rhs_codes.bitcast(FP8X4),
+                rhs_scale=rhs_scales,
+                start=start,
+                stop=stop,
+            )
+
+        y_acc = []
+        for t in range(PACK):
+            acc = psum.tile([P, S], F32, name="y_acc", tag="bank%d" % t)
+            product(acc[:], w1_codes, w1_scales, t, x1_words[:], x1_scales[:], True, True)
+            y_acc.append(acc)
+
+        ds_dealt = sb("ds_dealt", [P, S], U8)
+        nc.vector.tensor_copy(ds_dealt[:].rearrange("p (t m) -> p t m", t=PACK), ds_got[:].rearrange("p (m t) -> p t m", t=PACK))
+        l_n2 = load_list("l_n2", n2)
+        gk_sb = sb("gk_sb", [P, PACK], F32)
+        nc.sync.dma_start(gk_sb[:], gk.rearrange("(p t) o -> p (t o)", t=PACK))
+        for j in range(4):
+            nc.sync.dma_start(key_scales[j:P:32, :].bitcast(I32), ds_dealt[8 * j : P : 32, :].bitcast(I32))
+        l_n3 = load_list("l_n3", n3)
+        l_n4 = load_list("l_n4", n4)
+        w2_raw = load_weight("w2_raw", w2, 0, S)
+        l_n5 = load_list("l_n5", n5)
+        l_n6 = load_list("l_n6", n6)
+        l_n7 = load_list("l_n7", n7)
+
+        w3_bf = sb("w3_bf", [P, S, PACK], BF16)
+        for c in range(2):
+            nc.scalar.copy(weave(w3_bf[:, cols(c), :]), planes(w3_raw[c][:]))
+        x2_words = keep.tile([P, S], U32, name="x2_words", tag="w1_bf", align_bytes=64)
+        nc.vector.tensor_copy(x2_words[:], xw_tab[:].indirect(l_two[:]))
+        w3_codes = sb("w3_codes", [P, S], U32)
+        w3_scales = sb("w3_scales", [P, S], U8)
+        quantize(w3_codes, w3_scales, w3_bf, 0, S)
+        dw_got = sb("dw_got", [P, S], U32)
+        nc.vector.tensor_copy(dw_got[:], dw_tab[:].indirect(l_kidx[:]))
+        gk_full = sb("gk_full", [P, PACK], F32)
+        gk_half = sb("gk_half", [P, PACK], F32)
+        nc.vector.tensor_scalar(gk_full[:], gk_sb[:], 0.0625, None, ALU.mult)
+        nc.vector.tensor_scalar(gk_half[:], gk_sb[:], 0.03125, None, ALU.mult)
+        key_words = sb("key_words", [P, S], U32)
+        nc.vector.tensor_copy(
+            key_words[:].rearrange("p (t c i) -> p c t i", t=PACK, i=4), dw_got[:].rearrange("p (c i t) -> p c t i", t=PACK, i=4)
+        )
+        s_acc = []
+        for t in range(PACK):
+            acc = psum.tile([P, S], F32, name="s_acc", tag="bank%d" % (PACK + t))
+            product(acc[:], key_words, key_scales, t, x2_words[:], x2_scales[:], True, True)
+            s_acc.append(acc)
+
+        z_far = sb("z_far", [P, PACK, S], F32)
+        z_near = sb("z_near", [P, PACK, S], F32)
+        st = sb("st", [P, PACK, S], F32)
+        st_far = sb("st_far", [P, PACK, S], F32)
+
+        def z_tile(t):
+            sig_y = sb("sig_y%d" % t, [P, WIN], F32)
+            nc.scalar.activation(sig_y[:, :S], y_acc[t][:], ACT.Sigmoid)
+            yg = sb("yg%d" % t, [P, WIN], F32)
+            nc.scalar.activation(yg[:, :S], y_acc[t][:], ACT.Copy, scale=gn_sb[:, t : t + 1])
+            gate = sb("gate%d" % t, [P, S], F32)
+            nc.scalar.activation(gate[:], sig_y[:].indirect(l_n1[:]), ACT.Copy)
+            nc.vector.tensor_tensor(z_far[:, t, :], yg[:].indirect(l_n2[:]), gate[:], ALU.mult)
+            nc.vector.scalar_tensor_tensor(z_near[:, t, :], gate[:], 1.0, yg[:, :S], ALU.subtract, ALU.mult)
+
+        def st_pair(ts, halve_on_vector):
+            s_full = {}
+            s_half = {}
+            for t in ts:
+                s_full[t] = sb("s_full%d" % t, [P, S], F32)
+                s_half[t] = sb("s_half%d" % t, [P, WIN], F32)
+                nc.scalar.activation(s_full[t][:], s_acc[t][:], ACT.Copy, scale=gk_full[:, t : t + 1])
+                if not halve_on_vector:
+                    nc.scalar.activation(s_half[t][:, :S], s_acc[t][:], ACT.Copy, scale=gk_half[:, t : t + 1])
+            if halve_on_vector:
+                for t in ts:
+                    nc.vector.tensor_scalar(s_half[t][:, :S], s_full[t][:], 0.5, None, ALU.mult)
+            for t in ts:
+                nc.vector.tensor_tensor(st[:, t, :], s_half[t][:].indirect(l_n3[:]), s_full[t][:], ALU.add)
+
+        z_tile(0)
+        z_tile(1)
+        st_pair((0, 1), True)
+        z_tile(2)
+        st_pair((2, 3), False)
+        z_tile(3)
+
+        z_bf = sb("z_bf", [P, S, PACK], BF16)
+        z_codes = sb("z_codes", [P, S], U32)
+        z_scales = sb("z_scales", [P, S], U8)
+        z2_bf = sb("z2_bf", [P, S, PACK], BF16)
+        z2_codes = sb("z2_codes", [P, S], U32)
+        z2_scales = sb("z2_scales", [P, S], U8)
+        w2_bf = sb("w2_bf", [P, S, PACK], BF16)
+        w2_codes = sb("w2_codes", [P, S], U32)
+        w2_scales = sb("w2_scales", [P, S], U8)
+
+        def round_z(c):
+            nc.vector.tensor_tensor(weave(z_bf[:, cols(c), :]), planes(z_far[:, :, cols(c)]), planes(z_near[:, :, cols(c)]), ALU.subtract)
+
+        def round_z2(c):
+            nc.vector.tensor_tensor(weave(z2_bf[:, cols(c), :]), planes(st[:, :, cols(c)]), planes(st_far[:, :, cols(c)]), ALU.subtract)
+
+        def fetch_st(c):
+            for t in range(PACK):
+                nc.scalar.activation(st_far[:, t, cols(c)], st[:, t, :].indirect(half_list(l_n4, c)), ACT.Copy)
+
+        h_acc = {}
+
+        def h_products(c):
+            for m in range(PACK):
+                acc = psum.tile([P, HALF], F32, name="h_acc", tag="bank%d" % (PACK * c + m))
+                product(acc[:], w2_codes, w2_scales, m, z_codes[:, cols(c)], z_scales[:, cols(c)], True, False)
+                product(acc[:], w3_codes, w3_scales, m, z2_codes[:, cols(c)], z2_scales[:, cols(c)], False, True)
+                h_acc[c, m] = acc
+
+        fetch_st(0)
+        round_z2(0)
+        round_z(0)
+        nc.scalar.copy(weave(w2_bf[:]), planes(w2_raw[:]))
+        quantize(z2_codes, z2_scales, z2_bf, 0, HALF)
+        quantize(z_codes, z_scales, z_bf, 0, HALF)
+        quantize(w2_codes, w2_scales, w2_bf, 0, S)
+        h_products(0)
+        fetch_st(1)
+        round_z(1)
+        round_z2(1)
+        quantize(z_codes, z_scales, z_bf, HALF, S)
+        quantize(z2_codes, z2_scales, z2_bf, HALF, S)
+        h_products(1)
+
+        h = [sb("h%d" % m, [P, WIN], F32) for m in range(PACK)]
+        sig_h = [sb("sig_h%d" % m, [P, S], F32) for m in range(PACK)]
+        left = [sb("left%d" % m, [P, S], F32) for m in range(PACK)]
+        right = [sb("right%d" % m, [P, S], F32) for m in range(PACK)]
+
+        def leave(c, m):
+            if (c, m) == (1, 0):
+                nc.vector.tensor_copy(h[m][:, cols(c)], h_acc[c, m][:])
+            else:
+                nc.scalar.copy(h[m][:, cols(c)], h_acc[c, m][:])
+            nc.scalar.activation(sig_h[m][:, cols(c)], h_acc[c, m][:], ACT.Sigmoid)
+
+        def finish(m, pieces):
+            res = ring.tile([P, S], F32, name="res")
+            for c0, c1 in pieces:
+                nc.vector.tensor_tensor(res[:, c0:c1], left[m][:, c0:c1], right[m][:, c0:c1], ALU.add)
+                nc.sync.dma_start(out[m * P : (m + 1) * P, c0:c1], res[:, c0:c1])
+
+        for m in range(PACK):
+            leave(0, m)
+        for m in range(PACK):
+            leave(1, m)
+            gate7 = ring.tile([P, S], F32, name="gate7")
+            nc.scalar.activation(gate7[:], h[m][:].indirect(l_n7[:]), ACT.Sigmoid)
+            if m >= 2:
+                h6 = ring.tile([P, S], F32, name="h6")
+                nc.scalar.activation(h6[:], h[m][:].indirect(l_n6[:]), ACT.Copy)
+            nc.vector.tensor_tensor(left[m][:], h[m][:].indirect(l_n5[:]), sig_h[m][:], ALU.mult)
+            if m > 0:
+                finish(m - 1, [(0, S)])
+            if m >= 2:
+                nc.vector.tensor_tensor(right[m][:], h6[:], gate7[:], ALU.mult)
+            else:
+                nc.vector.tensor_tensor(right[m][:], h[m][:].indirect(l_n6[:]), gate7[:], ALU.mult)
+        finish(PACK - 1, [(0, HALF), (HALF, S)])

@@ -35,8 +35,8 @@ def tile_picked_jkeytrackhopwsum_none_p_kernel(
         ring = ctx.enter_context(tc.tile_pool(name="ring", bufs=2))
         psum = ctx.enter_context(tc.psum_pool(name="psum", bufs=1))
 
-        def sb(name, shape, dtype):
-            return keep.tile(shape, dtype, name=name, align_bytes=64)
+        def sb(name, shape, dtype, tag=None):
+            return keep.tile(shape, dtype, name=name, tag=tag or name, align_bytes=64)
 
         def load_list(name, src):
             t = lists.tile([P, LIST_COLS], U16, name=name)
@@ -49,8 +49,8 @@ def tile_picked_jkeytrackhopwsum_none_p_kernel(
         def half_list(lst, c):
             return lst[:, c * (LIST_COLS // 2) : (c + 1) * (LIST_COLS // 2)]
 
-        def load_weight(name, w, c0, c1):
-            raw = sb(name, [P, PACK, c1 - c0], F32)
+        def load_weight(name, w, c0, c1, tag=None):
+            raw = keep.tile([P, PACK, c1 - c0], F32, name=name, tag=tag or name, align_bytes=64)
             nc.sync.dma_start(raw[:], w.rearrange("(p j) n -> p j n", j=PACK)[:, :, c0:c1])
             return raw
 
@@ -119,22 +119,26 @@ def tile_picked_jkeytrackhopwsum_none_p_kernel(
                 stop=stop,
             )
 
-        y_acc = []
-        for t in range(PACK):
-            acc = psum.tile([P, S], F32, name="y_acc", tag="bank%d" % t)
-            product(acc[:], w1_codes, w1_scales, t, x1_words[:], x1_scales[:], True, True)
-            y_acc.append(acc)
+        def bank(number, width):
+            return psum.tile([P, width], F32, name="acc", tag="bank%d" % number)
+
+        y_acc = {}
+
+        def y_product(t, number):
+            y_acc[t] = bank(number, S)
+            product(y_acc[t][:], w1_codes, w1_scales, t, x1_words[:], x1_scales[:], True, True)
+
+        y_product(0, 0)
 
         ds_dealt = sb("ds_dealt", [P, S], U8)
         nc.vector.tensor_copy(ds_dealt[:].rearrange("p (t m) -> p t m", t=PACK), ds_got[:].rearrange("p (m t) -> p t m", t=PACK))
         l_n2 = load_list("l_n2", n2)
         gk_sb = sb("gk_sb", [P, PACK], F32)
         nc.sync.dma_start(gk_sb[:], gk.rearrange("(p t) o -> p (t o)", t=PACK))
-        for j in range(4):
-            nc.sync.dma_start(key_scales[j:P:32, :].bitcast(I32), ds_dealt[8 * j : P : 32, :].bitcast(I32))
+        for q in range(4):
+            nc.sync.dma_start(key_scales[32 * q : 32 * q + 4, :].bitcast(I32), ds_dealt[32 * q : 32 * q + 32 : 8, :].bitcast(I32))
         l_n3 = load_list("l_n3", n3)
         l_n4 = load_list("l_n4", n4)
-        w2_raw = load_weight("w2_raw", w2, 0, S)
         l_n5 = load_list("l_n5", n5)
         l_n6 = load_list("l_n6", n6)
         l_n7 = load_list("l_n7", n7)
@@ -151,27 +155,27 @@ def tile_picked_jkeytrackhopwsum_none_p_kernel(
         nc.vector.tensor_copy(dw_got[:], dw_tab[:].indirect(l_kidx[:]))
         gk_full = sb("gk_full", [P, PACK], F32)
         gk_half = sb("gk_half", [P, PACK], F32)
-        nc.vector.tensor_scalar(gk_full[:], gk_sb[:], 0.0625, None, ALU.mult)
-        nc.vector.tensor_scalar(gk_half[:], gk_sb[:], 0.03125, None, ALU.mult)
+        nc.gpsimd.tensor_scalar(gk_full[:], gk_sb[:], 0.0625, None, ALU.mult)
+        nc.gpsimd.tensor_scalar(gk_half[:], gk_sb[:], 0.03125, None, ALU.mult)
         key_words = sb("key_words", [P, S], U32)
         nc.vector.tensor_copy(
             key_words[:].rearrange("p (t c i) -> p c t i", t=PACK, i=4), dw_got[:].rearrange("p (c i t) -> p c t i", t=PACK, i=4)
         )
-        s_acc = []
-        for t in range(PACK):
-            acc = psum.tile([P, S], F32, name="s_acc", tag="bank%d" % (PACK + t))
-            product(acc[:], key_words, key_scales, t, x2_words[:], x2_scales[:], True, True)
-            s_acc.append(acc)
+        w2_raw = load_weight("w2_raw", w2, 0, S, "xw_tab")
+        s_acc = {}
 
-        z_far = sb("z_far", [P, PACK, S], F32)
-        z_near = sb("z_near", [P, PACK, S], F32)
+        def s_product(t, number):
+            s_acc[t] = bank(number, S)
+            product(s_acc[t][:], key_words, key_scales, t, x2_words[:], x2_scales[:], True, True)
+
+        z_far = sb("z_far", [P, PACK, S], F32, "dw_got")
+        z_near = sb("z_near", [P, PACK, S], F32, "dw_tab")
         st = sb("st", [P, PACK, S], F32)
-        st_far = sb("st_far", [P, PACK, S], F32)
 
         def z_tile(t):
-            sig_y = sb("sig_y%d" % t, [P, WIN], F32)
+            sig_y = sb("sig_y%d" % t, [P, WIN], F32, "w3_raw1" if t == 0 else None)
             nc.scalar.activation(sig_y[:, :S], y_acc[t][:], ACT.Sigmoid)
-            yg = sb("yg%d" % t, [P, WIN], F32)
+            yg = sb("yg%d" % t, [P, WIN], F32, "w3_raw0" if t == 0 else None)
             nc.scalar.activation(yg[:, :S], y_acc[t][:], ACT.Copy, scale=gn_sb[:, t : t + 1])
             gate = sb("gate%d" % t, [P, S], F32)
             nc.scalar.activation(gate[:], sig_y[:].indirect(l_n1[:]), ACT.Copy)
@@ -194,10 +198,17 @@ def tile_picked_jkeytrackhopwsum_none_p_kernel(
                 nc.vector.tensor_tensor(st[:, t, :], s_half[t][:].indirect(l_n3[:]), s_full[t][:], ALU.add)
 
         z_tile(0)
+        y_product(1, 0)
         z_tile(1)
+        s_product(0, 2)
+        s_product(1, 3)
         st_pair((0, 1), True)
+        y_product(2, 2)
         z_tile(2)
-        st_pair((2, 3), False)
+        s_product(2, 2)
+        s_product(3, 3)
+        st_pair((2, 3), True)
+        y_product(3, 2)
         z_tile(3)
 
         z_bf = sb("z_bf", [P, S, PACK], BF16)
@@ -206,7 +217,8 @@ def tile_picked_jkeytrackhopwsum_none_p_kernel(
         z2_bf = sb("z2_bf", [P, S, PACK], BF16)
         z2_codes = sb("z2_codes", [P, S], U32)
         z2_scales = sb("z2_scales", [P, S], U8)
-        w2_bf = sb("w2_bf", [P, S, PACK], BF16)
+        w2_bf = sb("w2_bf", [P, S, PACK], BF16, "gate3")
+        st_far = {}
         w2_codes = sb("w2_codes", [P, S], U32)
         w2_scales = sb("w2_scales", [P, S], U8)
 
@@ -214,17 +226,18 @@ def tile_picked_jkeytrackhopwsum_none_p_kernel(
             nc.vector.tensor_tensor(weave(z_bf[:, cols(c), :]), planes(z_far[:, :, cols(c)]), planes(z_near[:, :, cols(c)]), ALU.subtract)
 
         def round_z2(c):
-            nc.vector.tensor_tensor(weave(z2_bf[:, cols(c), :]), planes(st[:, :, cols(c)]), planes(st_far[:, :, cols(c)]), ALU.subtract)
+            nc.vector.tensor_tensor(weave(z2_bf[:, cols(c), :]), planes(st[:, :, cols(c)]), planes(st_far[c][:]), ALU.subtract)
 
         def fetch_st(c):
+            st_far[c] = sb("st_far%d" % c, [P, PACK, HALF], F32, ("sig_y3", "xw_tab")[c])
             for t in range(PACK):
-                nc.scalar.activation(st_far[:, t, cols(c)], st[:, t, :].indirect(half_list(l_n4, c)), ACT.Copy)
+                nc.scalar.activation(st_far[c][:, t, :], st[:, t, :].indirect(half_list(l_n4, c)), ACT.Copy)
 
         h_acc = {}
 
         def h_products(c):
             for m in range(PACK):
-                acc = psum.tile([P, HALF], F32, name="h_acc", tag="bank%d" % (PACK * c + m))
+                acc = bank(PACK * (1 - c) + m, HALF)
                 product(acc[:], w2_codes, w2_scales, m, z_codes[:, cols(c)], z_scales[:, cols(c)], True, False)
                 product(acc[:], w3_codes, w3_scales, m, z2_codes[:, cols(c)], z2_scales[:, cols(c)], False, True)
                 h_acc[c, m] = acc

@@ -62,10 +62,10 @@ def tile_picked_jkeytrackhopwsum_none_p_kernel(
             )
 
         def weave(grouped):
-            return grouped.rearrange("p (c i) t -> p c t i", i=4)
+            return grouped.rearrange("p (c i) t -> p c t i", i=2)
 
         def planes(four):
-            return four.rearrange("p t (c i) -> p c t i", i=4)
+            return four.rearrange("p t (c i) -> p c t i", i=2)
 
         ds_tab = sb("ds_tab", [P, G], U8)
         xs_tab = sb("xs_tab", [P, T], U8)
@@ -176,9 +176,12 @@ def tile_picked_jkeytrackhopwsum_none_p_kernel(
             sig_y = sb("sig_y%d" % t, [P, WIN], F32, "w3_raw1" if t == 0 else None)
             nc.scalar.activation(sig_y[:, :S], y_acc[t][:], ACT.Sigmoid)
             yg = sb("yg%d" % t, [P, WIN], F32, "w3_raw0" if t == 0 else None)
-            nc.scalar.activation(yg[:, :S], y_acc[t][:], ACT.Copy, scale=gn_sb[:, t : t + 1])
             gate = sb("gate%d" % t, [P, S], F32)
+            if t != 1:
+                nc.scalar.activation(yg[:, :S], y_acc[t][:], ACT.Copy, scale=gn_sb[:, t : t + 1])
             nc.scalar.activation(gate[:], sig_y[:].indirect(l_n1[:]), ACT.Copy)
+            if t == 1:
+                nc.vector.tensor_scalar(yg[:, :S], y_acc[t][:], gn_sb[:, t : t + 1], None, ALU.mult)
             nc.vector.tensor_tensor(z_far[:, t, :], yg[:].indirect(l_n2[:]), gate[:], ALU.mult)
             nc.vector.scalar_tensor_tensor(z_near[:, t, :], gate[:], 1.0, yg[:, :S], ALU.subtract, ALU.mult)
 
@@ -202,7 +205,7 @@ def tile_picked_jkeytrackhopwsum_none_p_kernel(
         z_tile(1)
         s_product(0, 2)
         s_product(1, 3)
-        st_pair((0, 1), True)
+        st_pair((0, 1), False)
         y_product(2, 2)
         z_tile(2)
         s_product(2, 2)
@@ -263,7 +266,7 @@ def tile_picked_jkeytrackhopwsum_none_p_kernel(
         right = [sb("right%d" % m, [P, S], F32) for m in range(PACK)]
 
         def leave(c, m):
-            if (c, m) == (1, 0):
+            if (c, m) in ((0, 3), (1, 0)):
                 nc.vector.tensor_copy(h[m][:, cols(c)], h_acc[c, m][:])
             else:
                 nc.scalar.copy(h[m][:, cols(c)], h_acc[c, m][:])

@@ -67,6 +67,10 @@ def tile_picked_jkeytrackhopwsum_none_p_kernel(
         def planes(four):
             return four.rearrange("p t (c i) -> p c t i", i=2)
 
+        warm = sb("warm", [P, 8], F32)
+        nc.vector.memset(warm[:, 0:1], 0.0)
+        nc.scalar.activation(warm[:, 1:2], warm[:, 0:1], ACT.Sigmoid)
+
         ds_tab = sb("ds_tab", [P, G], U8)
         xs_tab = sb("xs_tab", [P, T], U8)
         key_scales = sb("key_scales", [P, S], U8)

from contextlib import ExitStack

import concourse.mybir as mybir

F32 = mybir.dt.float32
BF16 = mybir.dt.bfloat16
I32 = mybir.dt.int32
U32 = mybir.dt.uint32
U16 = mybir.dt.uint16
U8 = mybir.dt.uint8
FP8X4 = mybir.dt.float8_e4m3fn_x4
ACT = mybir.ActivationFunctionType
ALU = mybir.AluOpType

P = 128
PACK = 4
K = 512
T = 1024
G = 2048
S = 512
HALF = S // 2
WIN = 2 * S
LIST_COLS = S // 16

FLOPS = 4 * 2 * 512 * 512 * 512


def tile_picked_jkeytrackhopwsum_none_p_kernel(
    tc, x_words, x_scales, w1, d_words, d_scales, gn, gk, w2, w3, offs, kidx, two, n1, n2, n3, n4, n5, n6, n7, out
):
    nc = tc.nc
    with ExitStack() as ctx:
        lists = ctx.enter_context(tc.tile_pool(name="lists", bufs=1))
        keep = ctx.enter_context(tc.tile_pool(name="keep", bufs=1))
        ring = ctx.enter_context(tc.tile_pool(name="ring", bufs=2))
        psum = ctx.enter_context(tc.psum_pool(name="psum", bufs=1))

        def sb(name, shape, dtype, tag=None):
            return keep.tile(shape, dtype, name=name, tag=tag or name, align_bytes=64)

        def load_list(name, src):
            t = lists.tile([P, LIST_COLS], U16, name=name)
            nc.sync.dma_start(t[:], src)
            return t

        def cols(c):
            return slice(c * HALF, (c + 1) * HALF)

        def half_list(lst, c):
            return lst[:, c * (LIST_COLS // 2) : (c + 1) * (LIST_COLS // 2)]

        def load_weight(name, w, c0, c1, tag=None):
            raw = keep.tile([P, PACK, c1 - c0], F32, name=name, tag=tag or name, align_bytes=64)
            nc.sync.dma_start(raw[:], w.rearrange("(p j) n -> p j n", j=PACK)[:, :, c0:c1])
            return raw

        def quantize(codes, scales, grouped, c0, c1):
            nc.vector.quantize_mx(
                out=codes[:, c0:c1].bitcast(FP8X4),
                scales=scales[:, c0:c1],
                in_=grouped[:, c0:c1, :].rearrange("p n j -> p (n j)"),
            )

        def weave(grouped):
            return grouped.rearrange("p (c i) t -> p c t i", i=2)

        def planes(four):
            return four.rearrange("p t (c i) -> p c t i", i=2)

        warm = sb("warm", [P, 8], F32)
        nc.vector.memset(warm[:, 0:1], 0.0)
        nc.scalar.activation(warm[:, 1:2], warm[:, 0:1], ACT.Sigmoid)

        ds_tab = sb("ds_tab", [P, G], U8)
        xs_tab = sb("xs_tab", [P, T], U8)
        key_scales = sb("key_scales", [P, S], U8)
        nc.gpsimd.memset(ds_tab[:].bitcast(I32), 0)
        nc.gpsimd.memset(key_scales[:].bitcast(I32), 0)

        l_offs = load_list("l_offs", offs)
        for q in range(4):
            rows = x_scales[0, 4 * q : 4 * q + 4, :].bitcast(I32)
            nc.sync.dma_start(xs_tab[32 * q : 32 * q + 32, :].bitcast(I32), rows.partition_broadcast(8))
        l_two = load_list("l_two", two)
        w1_raw = [load_weight("w1_raw0", w1, 0, HALF)]
        xw_tab = sb("xw_tab", [P, T], U32)
        nc.sync.dma_start(xw_tab[:].bitcast(I32), x_words[0].rearrange("p n t -> p (n t)").bitcast(I32))
        w1_raw.append(load_weight("w1_raw1", w1, HALF, S))
        l_kidx = load_list("l_kidx", kidx)
        nc.sync.dma_start(ds_tab[0:P:8, :].bitcast(I32), d_scales[0].bitcast(I32))
        gn_sb = sb("gn_sb", [P, PACK], F32)
        nc.sync.dma_start(gn_sb[:], gn.rearrange("(p t) o -> p (t o)", t=PACK))
        l_n1 = load_list("l_n1", n1)
        w3_raw = [load_weight("w3_raw%d" % c, w3, c * HALF, (c + 1) * HALF) for c in range(2)]
        dw_tab = sb("dw_tab", [P, G], U32)
        nc.sync.dma_start(dw_tab[:].bitcast(I32), d_words[0].rearrange("p n t -> p (n t)").bitcast(I32))

        w1_bf = keep.tile([P, S, PACK], BF16, name="w1_bf", tag="w1_bf", align_bytes=64)
        w1_view = w1_bf[:].rearrange("p (t m) j -> p m j t", t=PACK)
        for c in range(2):
            nc.scalar.copy(w1_view[:, c * 64 : (c + 1) * 64], w1_raw[c][:].rearrange("p j (m t) -> p m j t", t=PACK))
        x1_scales = sb("x1_scales", [P, S], U8)
        nc.vector.tensor_copy(x1_scales[:], xs_tab[:].indirect(l_offs[:]))
        x2_scales = sb("x2_scales", [P, S], U8)
        nc.vector.tensor_copy(x2_scales[:], xs_tab[:].indirect(l_two[:]))
        x1_words = sb("x1_words", [P, S], U32)
        nc.vector.tensor_copy(x1_words[:], xw_tab[:].indirect(l_offs[:]))
        ds_got = sb("ds_got", [P, S], U8)
        nc.vector.tensor_copy(ds_got[:], ds_tab[:].indirect(l_kidx[:]))
        w1_codes = sb("w1_codes", [P, S], U32)
        w1_scales = sb("w1_scales", [P, S], U8)
        quantize(w1_codes, w1_scales, w1_bf, 0, S)

        def product(acc, lhs_codes, lhs_scales, t, rhs_codes, rhs_scales, start, stop):
            m = slice(t * P, (t + 1) * P)
            nc.tensor.matmul_mx(
                out=acc,
                lhsT=lhs_codes[:, m].bitcast(FP8X4),
                lhsT_scale=lhs_scales[:, m],
                rhs=rhs_codes.bitcast(FP8X4),
                rhs_scale=rhs_scales,
                start=start,
                stop=stop,
            )

        def bank(number, width):
            return psum.tile([P, width], F32, name="acc", tag="bank%d" % number)

        y_acc = {}

        def y_product(t, number):
            y_acc[t] = bank(number, S)
            product(y_acc[t][:], w1_codes, w1_scales, t, x1_words[:], x1_scales[:], True, True)

        y_product(0, 0)

        ds_dealt = sb("ds_dealt", [P, S], U8)
        nc.vector.tensor_copy(ds_dealt[:].rearrange("p (t m) -> p t m", t=PACK), ds_got[:].rearrange("p (m t) -> p t m", t=PACK))
        l_n2 = load_list("l_n2", n2)
        gk_sb = sb("gk_sb", [P, PACK], F32)
        nc.sync.dma_start(gk_sb[:], gk.rearrange("(p t) o -> p (t o)", t=PACK))
        for q in range(4):
            nc.sync.dma_start(key_scales[32 * q : 32 * q + 4, :].bitcast(I32), ds_dealt[32 * q : 32 * q + 32 : 8, :].bitcast(I32))
        l_n3 = load_list("l_n3", n3)
        l_n4 = load_list("l_n4", n4)
        l_n5 = load_list("l_n5", n5)
        l_n6 = load_list("l_n6", n6)
        l_n7 = load_list("l_n7", n7)

        w3_bf = sb("w3_bf", [P, S, PACK], BF16)
        for c in range(2):
            nc.scalar.copy(weave(w3_bf[:, cols(c), :]), planes(w3_raw[c][:]))
        x2_words = keep.tile([P, S], U32, name="x2_words", tag="w1_bf", align_bytes=64)
        nc.vector.tensor_copy(x2_words[:], xw_tab[:].indirect(l_two[:]))
        w3_codes = sb("w3_codes", [P, S], U32)
        w3_scales = sb("w3_scales", [P, S], U8)
        quantize(w3_codes, w3_scales, w3_bf, 0, S)
        dw_got = sb("dw_got", [P, S], U32)
        nc.vector.tensor_copy(dw_got[:], dw_tab[:].indirect(l_kidx[:]))
        gk_full = sb("gk_full", [P, PACK], F32)
        gk_half = sb("gk_half", [P, PACK], F32)
        nc.gpsimd.tensor_scalar(gk_full[:], gk_sb[:], 0.0625, None, ALU.mult)
        nc.gpsimd.tensor_scalar(gk_half[:], gk_sb[:], 0.03125, None, ALU.mult)
        key_words = sb("key_words", [P, S], U32)
        nc.vector.tensor_copy(
            key_words[:].rearrange("p (t c i) -> p c t i", t=PACK, i=4), dw_got[:].rearrange("p (c i t) -> p c t i", t=PACK, i=4)
        )
        w2_raw = load_weight("w2_raw", w2, 0, S, "xw_tab")
        s_acc = {}

        def s_product(t, number):
            s_acc[t] = bank(number, S)
            product(s_acc[t][:], key_words, key_scales, t, x2_words[:], x2_scales[:], True, True)

        z_far = sb("z_far", [P, PACK, S], F32, "dw_got")
        z_near = sb("z_near", [P, PACK, S], F32, "dw_tab")
        st = sb("st", [P, PACK, S], F32)

        def z_tile(t):
            sig_y = sb("sig_y%d" % t, [P, WIN], F32, "w3_raw1" if t == 0 else None)
            nc.scalar.activation(sig_y[:, :S], y_acc[t][:], ACT.Sigmoid)
            yg = sb("yg%d" % t, [P, WIN], F32, "w3_raw0" if t == 0 else None)
            gate = sb("gate%d" % t, [P, S], F32)
            if t != 1:
                nc.scalar.activation(yg[:, :S], y_acc[t][:], ACT.Copy, scale=gn_sb[:, t : t + 1])
            nc.scalar.activation(gate[:], sig_y[:].indirect(l_n1[:]), ACT.Copy)
            if t == 1:
                nc.vector.tensor_scalar(yg[:, :S], y_acc[t][:], gn_sb[:, t : t + 1], None, ALU.mult)
            nc.vector.tensor_tensor(z_far[:, t, :], yg[:].indirect(l_n2[:]), gate[:], ALU.mult)
            nc.vector.scalar_tensor_tensor(z_near[:, t, :], gate[:], 1.0, yg[:, :S], ALU.subtract, ALU.mult)

        def st_pair(ts, halve_on_vector):
            s_full = {}
            s_half = {}
            for t in ts:
                s_full[t] = sb("s_full%d" % t, [P, S], F32)
                s_half[t] = sb("s_half%d" % t, [P, WIN], F32)
                nc.scalar.activation(s_full[t][:], s_acc[t][:], ACT.Copy, scale=gk_full[:, t : t + 1])
                if not halve_on_vector:
                    nc.scalar.activation(s_half[t][:, :S], s_acc[t][:], ACT.Copy, scale=gk_half[:, t : t + 1])
            if halve_on_vector:
                for t in ts:
                    nc.vector.tensor_scalar(s_half[t][:, :S], s_full[t][:], 0.5, None, ALU.mult)
            for t in ts:
                nc.vector.tensor_tensor(st[:, t, :], s_half[t][:].indirect(l_n3[:]), s_full[t][:], ALU.add)

        z_tile(0)
        y_product(1, 0)
        z_tile(1)
        s_product(0, 2)
        s_product(1, 3)
        st_pair((0, 1), False)
        y_product(2, 2)
        z_tile(2)
        s_product(2, 2)
        s_product(3, 3)
        st_pair((2, 3), True)
        y_product(3, 2)
        z_tile(3)

        z_bf = sb("z_bf", [P, S, PACK], BF16)
        z_codes = sb("z_codes", [P, S], U32)
        z_scales = sb("z_scales", [P, S], U8)
        z2_bf = sb("z2_bf", [P, S, PACK], BF16)
        z2_codes = sb("z2_codes", [P, S], U32)
        z2_scales = sb("z2_scales", [P, S], U8)
        w2_bf = sb("w2_bf", [P, S, PACK], BF16, "gate3")
        st_far = {}
        w2_codes = sb("w2_codes", [P, S], U32)
        w2_scales = sb("w2_scales", [P, S], U8)

        def round_z(c):
            nc.vector.tensor_tensor(weave(z_bf[:, cols(c), :]), planes(z_far[:, :, cols(c)]), planes(z_near[:, :, cols(c)]), ALU.subtract)

        def round_z2(c):
            nc.vector.tensor_tensor(weave(z2_bf[:, cols(c), :]), planes(st[:, :, cols(c)]), planes(st_far[c][:]), ALU.subtract)

        def fetch_st(c):
            st_far[c] = sb("st_far%d" % c, [P, PACK, HALF], F32, ("sig_y3", "xw_tab")[c])
            for t in range(PACK):
                nc.scalar.activation(st_far[c][:, t, :], st[:, t, :].indirect(half_list(l_n4, c)), ACT.Copy)

        h_acc = {}

        def h_products(c):
            for m in range(PACK):
                acc = bank(PACK * (1 - c) + m, HALF)
                product(acc[:], w2_codes, w2_scales, m, z_codes[:, cols(c)], z_scales[:, cols(c)], True, False)
                product(acc[:], w3_codes, w3_scales, m, z2_codes[:, cols(c)], z2_scales[:, cols(c)], False, True)
                h_acc[c, m] = acc

        fetch_st(0)
        round_z2(0)
        round_z(0)
        nc.scalar.copy(weave(w2_bf[:]), planes(w2_raw[:]))
        quantize(z2_codes, z2_scales, z2_bf, 0, HALF)
        quantize(z_codes, z_scales, z_bf, 0, HALF)
        quantize(w2_codes, w2_scales, w2_bf, 0, S)
        h_products(0)
        fetch_st(1)
        round_z(1)
        round_z2(1)
        quantize(z_codes, z_scales, z_bf, HALF, S)
        quantize(z2_codes, z2_scales, z2_bf, HALF, S)
        h_products(1)

        h = [sb("h%d" % m, [P, WIN], F32) for m in range(PACK)]
        sig_h = [sb("sig_h%d" % m, [P, S], F32) for m in range(PACK)]
        left = [sb("left%d" % m, [P, S], F32) for m in range(PACK)]
        right = [sb("right%d" % m, [P, S], F32) for m in range(PACK)]

        def leave(c, m):
            if (c, m) in ((0, 3), (1, 0)):
                nc.vector.tensor_copy(h[m][:, cols(c)], h_acc[c, m][:])
            else:
                nc.scalar.copy(h[m][:, cols(c)], h_acc[c, m][:])
            nc.scalar.activation(sig_h[m][:, cols(c)], h_acc[c, m][:], ACT.Sigmoid)

        def finish(m, pieces):
            res = ring.tile([P, S], F32, name="res")
            for c0, c1 in pieces:
                nc.vector.tensor_tensor(res[:, c0:c1], left[m][:, c0:c1], right[m][:, c0:c1], ALU.add)
                nc.sync.dma_start(out[m * P : (m + 1) * P, c0:c1], res[:, c0:c1])

        for m in range(PACK):
            leave(0, m)
        for m in range(PACK):
            leave(1, m)
            gate7 = ring.tile([P, S], F32, name="gate7")
            nc.scalar.activation(gate7[:], h[m][:].indirect(l_n7[:]), ACT.Sigmoid)
            if m >= 2:
                h6 = ring.tile([P, S], F32, name="h6")
                nc.scalar.activation(h6[:], h[m][:].indirect(l_n6[:]), ACT.Copy)
            nc.vector.tensor_tensor(left[m][:], h[m][:].indirect(l_n5[:]), sig_h[m][:], ALU.mult)
            if m > 0:
                finish(m - 1, [(0, S)])
            if m >= 2:
                nc.vector.tensor_tensor(right[m][:], h6[:], gate7[:], ALU.mult)
            else:
                nc.vector.tensor_tensor(right[m][:], h[m][:].indirect(l_n6[:]), gate7[:], ALU.mult)
        finish(PACK - 1, [(0, HALF), (HALF, S)])
